import numpy as np
CORES = [8,9,10,11,12,13,14,15,16,17,18,19,20,21,22,23]
N = 16
COUNTS = [[0,4,4,4,0,32,4,0,0,4,4,0,0,4,0,0],[0,0,4,8,4,32,0,8,4,8,4,8,0,0,8,0],[4,4,0,0,0,32,0,8,0,8,0,8,0,8,0,0],[8,0,0,0,0,32,8,0,8,4,8,4,0,4,8,0],[0,8,4,4,0,32,8,4,8,8,8,8,8,8,4,4],[0,0,4,8,0,0,8,8,8,4,0,8,8,4,0,4],[8,4,8,4,4,32,0,0,4,8,4,4,4,8,8,8],[4,4,4,8,0,32,0,0,0,0,0,4,4,0,0,0],[8,4,8,4,8,32,0,4,0,0,4,4,4,4,4,0],[0,8,0,8,8,32,4,8,4,0,4,8,0,8,8,4],[0,4,4,4,8,32,0,4,0,0,0,8,4,8,0,8],[0,0,0,4,4,32,0,4,0,4,0,0,0,4,0,8],[0,4,0,4,0,32,0,8,8,8,4,0,0,0,8,4],[4,0,8,0,0,32,4,0,4,0,4,8,0,0,0,0],[8,0,0,4,8,32,0,4,4,8,8,8,8,0,0,4],[4,8,4,8,0,32,0,4,0,4,0,0,4,8,0,0]]
XW, YW = 116, 480
def setup_inputs(rng):
    return {"x": rng.standard_normal((N, 128, XW), dtype=np.float32)}
def reference(x):
    y = np.full((N, 128, YW), np.nan, x.dtype)
    fill = [0] * N
    for s in range(N):
        o = 0
        for d in range(N):
            c = COUNTS[s][d]
            y[d][:, fill[d]:fill[d] + c] = x[s][:, o:o + c]
            o += c; fill[d] += c
    return {"y": y}

@@ -1,0 +1,147 @@
+SCRATCH = {
+    "xs": ("sbuf", [128, 116], "float32"),
+    "stage": ("sbuf", [128, 128], "float32"),
+    "land": ("sbuf", [128, 480], "float32"),
+}
+SEMAPHORES = ["loaded", "staged", "arrived", "stored", "sent"]
+
+PLAN = {}
+
+
+def popcount(m):
+    return bin(m).count("1")
+
+
+def make_plan(counts, cores, topo):
+    n = len(cores)
+    chips = sorted(set(topo.chip(c) for c in cores))
+    route, soff = {}, {}
+    for X in chips:
+        for Y in chips:
+            if X == Y:
+                continue
+            M = Y ^ 1
+            srcs = [r for r in range(n) if topo.chip(cores[r]) == X]
+            dsts = [r for r in range(n) if topo.chip(cores[r]) == Y]
+            seq = [(s, d) for d in dsts for s in srcs if counts[s][d] > 0]
+            total = sum(counts[s][d] for s, d in seq)
+            chunks = [[] for _ in range(8)]
+            cum = 0
+            for s, d in seq:
+                c = counts[s][d]
+                k = min(7, int((cum + c / 2.0) * 8 / total))
+                chunks[k].append((s, d))
+                cum += c
+            size = [sum(counts[s][d] for s, d in ch) for ch in chunks]
+            bydie = [[sum(counts[s][d] for s, d in ch if topo.die(cores[s]) == e) for e in (0, 1)] for ch in chunks]
+            best = None
+            for hm in range(256):
+                if popcount(hm) != 4:
+                    continue
+                H = [k for k in range(8) if hm >> k & 1]
+                O = [k for k in range(8) if not hm >> k & 1]
+                sw = [sum(bydie[k][e] for k in H) for e in (0, 1)]
+                for a in range(1, 4):
+                    h1 = [H[0], H[a]]
+                    h0 = [k for k in H if k not in h1]
+                    for b in range(1, 4):
+                        o1 = [O[0], O[b]]
+                        o0 = [k for k in O if k not in o1]
+                        loads = sw + [sum(size[k] for k in grp) for grp in (h1, h0, o1, o0)]
+                        key = (max(loads), sum(v * v for v in loads))
+                        if best is None or key < best[0]:
+                            best = (key, o1, o0, h1, h0)
+            _, o1, o0, h1, h0 = best
+            fw = {o1[0]: X * 8 + 2, o1[1]: X * 8 + 3, o0[0]: X * 8 + 6, o0[1]: X * 8 + 7,
+                  h1[0]: M * 8 + 2, h1[1]: M * 8 + 3, h0[0]: M * 8 + 6, h0[1]: M * 8 + 7}
+            for k in range(8):
+                o = 0
+                for s, d in chunks[k]:
+                    route[(s, d)] = fw[k]
+                    soff[(s, d)] = o
+                    o += counts[s][d]
+    return route, soff
+
+
+def rank_program(g, core, T, topo):
+    counts = T.tables["COUNTS"]
+    cores = list(T.cores)
+    n = len(cores)
+    if "p" not in PLAN:
+        PLAN["p"] = make_plan(counts, cores, topo)
+    route, soff = PLAN["p"]
+    xoff = [[sum(counts[s][:d]) for d in range(n)] for s in range(n)]
+    yoff = [[sum(counts[t][d] for t in range(s)) for s in range(n)] for d in range(n)]
+    rank = T.rank_of(core)
+    sent = [0]
+
+    def write(dst, out_ap, in_ap, sem):
+        rid, pid, _ = topo.addr(dst)
+        m = topo.mask(core, dst)
+        g.remote_dma(out_ap, in_ap, sem, T.sem.sent, pid, rid, m)
+        sent[0] += popcount(m)
+
+    def engines(src, dst):
+        return popcount(topo.mask(src, dst))
+
+    mine = sorted([(d, s) for (s, d), f in route.items() if f == core])
+    staged = 0
+    for d, s in mine:
+        staged += 16 if cores[s] == core else engines(cores[s], core)
+
+    if rank is not None:
+        xt = sum(counts[rank])
+        g.sync.dma_start(T.xs[:, 0:xt], T.x[:, 0:xt]).then_inc(T.sem.loaded, 16)
+        for d, s in mine:
+            if s == rank:
+                c = counts[s][d]
+                g.scalar.dma_start(T.stage[:, soff[(s, d)]:soff[(s, d)] + c],
+                                   T.x[:, xoff[s][d]:xoff[s][d] + c]).then_inc(T.sem.staged, 16)
+        c = counts[rank][rank]
+        if c:
+            g.scalar.dma_start(T.land[:, yoff[rank][rank]:yoff[rank][rank] + c],
+                               T.x[:, xoff[rank][rank]:xoff[rank][rank] + c]).then_inc(T.sem.arrived, 16)
+        g.wait_ge(T.sem.loaded, 16)
+        for d in range(n):
+            c = counts[rank][d]
+            if c == 0 or d == rank:
+                continue
+            src = T.xs[:, xoff[rank][d]:xoff[rank][d] + c]
+            if (rank, d) in route:
+                f = route[(rank, d)]
+                if f != core:
+                    write(f, T.stage[:, soff[(rank, d)]:soff[(rank, d)] + c], src, T.sem.staged)
+            else:
+                write(cores[d], T.land[:, yoff[d][rank]:yoff[d][rank] + c], src, T.sem.arrived)
+
+    def runs_of(f):
+        ps = sorted([(d, s) for (s, d), ff in route.items() if ff == f])
+        runs = []
+        for d, s in ps:
+            c = counts[s][d]
+            if runs and runs[-1][0] == d and runs[-1][1] + runs[-1][3] == yoff[d][s]:
+                runs[-1][3] += c
+            else:
+                runs.append([d, yoff[d][s], soff[(s, d)], c])
+        return runs
+
+    if mine:
+        g.wait_ge(T.sem.staged, staged)
+        for d, yo, so, c in runs_of(core):
+            write(cores[d], T.land[:, yo:yo + c], T.stage[:, so:so + c], T.sem.arrived)
+
+    if rank is not None:
+        arrived = 16 if counts[rank][rank] else 0
+        for s in range(n):
+            if s != rank and counts[s][rank] and (s, rank) not in route:
+                arrived += engines(cores[s], core)
+        for f in sorted(set(route.values())):
+            for d, yo, so, c in runs_of(f):
+                if d == rank:
+                    arrived += engines(f, core)
+        yt = sum(counts[s][rank] for s in range(n))
+        g.wait_ge(T.sem.arrived, arrived)
+        g.dma_start(T.y[:, 0:yt], T.land[:, 0:yt]).then_inc(T.sem.stored, 16)
+        g.wait_ge(T.sem.stored, 16)
+    if sent[0]:
+        g.wait_ge(T.sem.sent, sent[0])

@@ -1,147 +1,150 @@
+from concourse.bass import DstId, RemoteDMATransfer
+
 SCRATCH = {
     "xs": ("sbuf", [128, 116], "float32"),
-    "stage": ("sbuf", [128, 128], "float32"),
+    "stage": ("sbuf", [128, 88], "float32"),
     "land": ("sbuf", [128, 480], "float32"),
 }
 SEMAPHORES = ["loaded", "staged", "arrived", "stored", "sent"]
 
-PLAN = {}
+RELAYS = (
+    (2, ((8, 3, 5), (9, 5, 7))),
+    (3, ((8, 0, 2), (8, 7, 7))),
+    (6, ((12, 1, 5), (13, 5, 6))),
+    (7, ((12, 7, 7), (13, 0, 2), (15, 0, 2))),
+    (24, ((10, 5, 5), (11, 5, 7))),
+    (25, ((10, 1, 2), (10, 7, 7), (11, 3, 4))),
+    (28, ((14, 0, 5), (15, 5, 7))),
+    (29, ((14, 7, 7), (15, 3, 3))),
+    (19, ((9, 1, 4),)),
+    (23, ((10, 3, 4),)),
+    (26, ((0, 9, 13), (3, 11, 14))),
+    (27, ((1, 8, 14),)),
+    (30, ((4, 8, 11),)),
+    (31, ((4, 12, 15), (5, 8, 8))),
+    (0, ((2, 9, 13),)),
+    (1, ((3, 8, 10),)),
+    (4, ((6, 8, 11), (7, 11, 12))),
+    (5, ((6, 12, 15),)),
+    (10, ((5, 9, 12),)),
+    (15, ((5, 13, 15),)),
+)
+
+CACHE = {}
 
 
-def popcount(m):
-    return bin(m).count("1")
+def pack(writes, src, topo):
+    groups = []
+    for w in writes:
+        key = (topo.chip(w[0]) != topo.chip(src), w[5])
+        for grp in groups:
+            if grp[0] == key:
+                grp[1].append(w)
+                break
+        else:
+            groups.append((key, [w]))
+    calls = []
+    for (off, _), ws in groups:
+        cap = 8 if off else 16
+        while ws:
+            k = 1
+            while k * 2 <= min(len(ws), 8):
+                k *= 2
+            e = cap // k
+            calls.append([(w, ((1 << e) - 1) << (i * e)) for i, w in enumerate(ws[:k])])
+            ws = ws[k:]
+    return calls
 
 
-def make_plan(counts, cores, topo):
+def build(counts, cores, topo):
     n = len(cores)
-    chips = sorted(set(topo.chip(c) for c in cores))
-    route, soff = {}, {}
-    for X in chips:
-        for Y in chips:
-            if X == Y:
-                continue
-            M = Y ^ 1
-            srcs = [r for r in range(n) if topo.chip(cores[r]) == X]
-            dsts = [r for r in range(n) if topo.chip(cores[r]) == Y]
-            seq = [(s, d) for d in dsts for s in srcs if counts[s][d] > 0]
-            total = sum(counts[s][d] for s, d in seq)
-            chunks = [[] for _ in range(8)]
-            cum = 0
-            for s, d in seq:
+    xoff = [[sum(counts[s][:d]) for d in range(n)] for s in range(n)]
+    yoff = [[sum(counts[q][d] for q in range(s)) for s in range(n)] for d in range(n)]
+    seg_w = {c: [] for c in range(32)}
+    own_w = {c: [] for c in range(32)}
+    out_w = {c: [] for c in range(32)}
+    todo = set((s, d) for s in range(n) for d in range(n)
+               if counts[s][d] and topo.chip(cores[s]) != topo.chip(cores[d]))
+    for s in range(n):
+        for d in range(n):
+            if counts[s][d] and s != d and (s, d) not in todo:
+                own_w[cores[s]].append([cores[d], "land", yoff[d][s], "xs", xoff[s][d], counts[s][d], "arrived"])
+    for relay, segs in RELAYS:
+        col = 0
+        for s, a, b in segs:
+            width = sum(counts[s][a:b + 1])
+            seg_w[cores[s]].append([relay, "stage", col, "xs", xoff[s][a], width, "staged"])
+            for d in range(a, b + 1):
                 c = counts[s][d]
-                k = min(7, int((cum + c / 2.0) * 8 / total))
-                chunks[k].append((s, d))
-                cum += c
-            size = [sum(counts[s][d] for s, d in ch) for ch in chunks]
-            bydie = [[sum(counts[s][d] for s, d in ch if topo.die(cores[s]) == e) for e in (0, 1)] for ch in chunks]
-            best = None
-            for hm in range(256):
-                if popcount(hm) != 4:
+                if c == 0:
                     continue
-                H = [k for k in range(8) if hm >> k & 1]
-                O = [k for k in range(8) if not hm >> k & 1]
-                sw = [sum(bydie[k][e] for k in H) for e in (0, 1)]
-                for a in range(1, 4):
-                    h1 = [H[0], H[a]]
-                    h0 = [k for k in H if k not in h1]
-                    for b in range(1, 4):
-                        o1 = [O[0], O[b]]
-                        o0 = [k for k in O if k not in o1]
-                        loads = sw + [sum(size[k] for k in grp) for grp in (h1, h0, o1, o0)]
-                        key = (max(loads), sum(v * v for v in loads))
-                        if best is None or key < best[0]:
-                            best = (key, o1, o0, h1, h0)
-            _, o1, o0, h1, h0 = best
-            fw = {o1[0]: X * 8 + 2, o1[1]: X * 8 + 3, o0[0]: X * 8 + 6, o0[1]: X * 8 + 7,
-                  h1[0]: M * 8 + 2, h1[1]: M * 8 + 3, h0[0]: M * 8 + 6, h0[1]: M * 8 + 7}
-            for k in range(8):
-                o = 0
-                for s, d in chunks[k]:
-                    route[(s, d)] = fw[k]
-                    soff[(s, d)] = o
-                    o += counts[s][d]
-    return route, soff
+                todo.remove((s, d))
+                last = out_w[relay][-1] if out_w[relay] else None
+                if last and last[0] == cores[d] and last[2] + last[5] == yoff[d][s] and last[4] + last[5] == col:
+                    last[5] += c
+                else:
+                    out_w[relay].append([cores[d], "land", yoff[d][s], "stage", col, c, "arrived"])
+                col += c
+    if todo:
+        raise ValueError("RELAYS leaves pieces out: %s" % sorted(todo))
+    first, second = {}, {}
+    expect = {c: {"staged": 0, "arrived": 0, "sent": 0} for c in range(32)}
+    for c in range(32):
+        first[c] = pack(seg_w[c], c, topo) + pack(own_w[c], c, topo)
+        second[c] = pack(out_w[c], c, topo)
+        for call in first[c] + second[c]:
+            for w, mask in call:
+                e = bin(mask).count("1")
+                expect[w[0]][w[6]] += e
+                expect[c]["sent"] += e
+    return first, second, expect, xoff, yoff
 
 
 def rank_program(g, core, T, topo):
     counts = T.tables["COUNTS"]
     cores = list(T.cores)
     n = len(cores)
-    if "p" not in PLAN:
-        PLAN["p"] = make_plan(counts, cores, topo)
-    route, soff = PLAN["p"]
-    xoff = [[sum(counts[s][:d]) for d in range(n)] for s in range(n)]
-    yoff = [[sum(counts[t][d] for t in range(s)) for s in range(n)] for d in range(n)]
+    if "plan" not in CACHE:
+        CACHE["plan"] = build(counts, cores, topo)
+    first, second, expect, xoff, yoff = CACHE["plan"]
     rank = T.rank_of(core)
-    sent = [0]
+    arrived = expect[core]["arrived"]
 
-    def write(dst, out_ap, in_ap, sem):
-        rid, pid, _ = topo.addr(dst)
-        m = topo.mask(core, dst)
-        g.remote_dma(out_ap, in_ap, sem, T.sem.sent, pid, rid, m)
-        sent[0] += popcount(m)
-
-    def engines(src, dst):
-        return popcount(topo.mask(src, dst))
-
-    mine = sorted([(d, s) for (s, d), f in route.items() if f == core])
-    staged = 0
-    for d, s in mine:
-        staged += 16 if cores[s] == core else engines(cores[s], core)
+    def issue(calls):
+        for call in calls:
+            if len(call) == 1:
+                (dst, ob, oc, ib, ic, width, sem), mask = call[0]
+                rid, pid, _ = topo.addr(dst)
+                g.remote_dma(T[ob][:, oc:oc + width], T[ib][:, ic:ic + width], T.sem[sem], T.sem.sent, pid, rid, mask)
+                continue
+            transfers = []
+            for (dst, ob, oc, ib, ic, width, sem), mask in call:
+                rid, pid, _ = topo.addr(dst)
+                transfers.append(RemoteDMATransfer(dst_ids=[DstId(rid=rid, pnc=pid)], dma_engine_mask=mask,
+                                                   remote_sem=T.sem[sem], src=T[ib][:, ic:ic + width],
+                                                   dst=T[ob][:, oc:oc + width]))
+            g.remote_dma_fused(transfers, local_sem=T.sem.sent)
 
     if rank is not None:
-        xt = sum(counts[rank])
-        g.sync.dma_start(T.xs[:, 0:xt], T.x[:, 0:xt]).then_inc(T.sem.loaded, 16)
-        for d, s in mine:
-            if s == rank:
-                c = counts[s][d]
-                g.scalar.dma_start(T.stage[:, soff[(s, d)]:soff[(s, d)] + c],
-                                   T.x[:, xoff[s][d]:xoff[s][d] + c]).then_inc(T.sem.staged, 16)
+        used = sum(counts[rank])
+        g.sync.dma_start(T.xs[:, 0:used], T.x[:, 0:used]).then_inc(T.sem.loaded, 16)
         c = counts[rank][rank]
         if c:
             g.scalar.dma_start(T.land[:, yoff[rank][rank]:yoff[rank][rank] + c],
                                T.x[:, xoff[rank][rank]:xoff[rank][rank] + c]).then_inc(T.sem.arrived, 16)
+            arrived += 16
         g.wait_ge(T.sem.loaded, 16)
-        for d in range(n):
-            c = counts[rank][d]
-            if c == 0 or d == rank:
-                continue
-            src = T.xs[:, xoff[rank][d]:xoff[rank][d] + c]
-            if (rank, d) in route:
-                f = route[(rank, d)]
-                if f != core:
-                    write(f, T.stage[:, soff[(rank, d)]:soff[(rank, d)] + c], src, T.sem.staged)
-            else:
-                write(cores[d], T.land[:, yoff[d][rank]:yoff[d][rank] + c], src, T.sem.arrived)
+        issue(first[core])
 
-    def runs_of(f):
-        ps = sorted([(d, s) for (s, d), ff in route.items() if ff == f])
-        runs = []
-        for d, s in ps:
-            c = counts[s][d]
-            if runs and runs[-1][0] == d and runs[-1][1] + runs[-1][3] == yoff[d][s]:
-                runs[-1][3] += c
-            else:
-                runs.append([d, yoff[d][s], soff[(s, d)], c])
-        return runs
-
-    if mine:
-        g.wait_ge(T.sem.staged, staged)
-        for d, yo, so, c in runs_of(core):
-            write(cores[d], T.land[:, yo:yo + c], T.stage[:, so:so + c], T.sem.arrived)
+    if second[core]:
+        g.wait_ge(T.sem.staged, expect[core]["staged"])
+        issue(second[core])
 
     if rank is not None:
-        arrived = 16 if counts[rank][rank] else 0
-        for s in range(n):
-            if s != rank and counts[s][rank] and (s, rank) not in route:
-                arrived += engines(cores[s], core)
-        for f in sorted(set(route.values())):
-            for d, yo, so, c in runs_of(f):
-                if d == rank:
-                    arrived += engines(f, core)
-        yt = sum(counts[s][rank] for s in range(n))
+        owed = sum(counts[s][rank] for s in range(n))
         g.wait_ge(T.sem.arrived, arrived)
-        g.dma_start(T.y[:, 0:yt], T.land[:, 0:yt]).then_inc(T.sem.stored, 16)
+        g.dma_start(T.y[:, 0:owed], T.land[:, 0:owed]).then_inc(T.sem.stored, 16)
         g.wait_ge(T.sem.stored, 16)
-    if sent[0]:
-        g.wait_ge(T.sem.sent, sent[0])
+
+    if expect[core]["sent"]:
+        g.wait_ge(T.sem.sent, expect[core]["sent"])

@@ -11,13 +11,13 @@ RELAYS = (
     (2, ((8, 3, 5), (9, 5, 7))),
     (3, ((8, 0, 2), (8, 7, 7))),
     (6, ((12, 1, 5), (13, 5, 6))),
-    (7, ((12, 7, 7), (13, 0, 2), (15, 0, 2))),
+    (7, ((12, 7, 7), (14, 7, 7), (13, 0, 2), (15, 0, 1))),
     (24, ((10, 5, 5), (11, 5, 7))),
-    (25, ((10, 1, 2), (10, 7, 7), (11, 3, 4))),
+    (25, ((10, 1, 3), (11, 3, 4))),
     (28, ((14, 0, 5), (15, 5, 7))),
-    (29, ((14, 7, 7), (15, 3, 3))),
+    (29, ((15, 2, 3),)),
     (19, ((9, 1, 4),)),
-    (23, ((10, 3, 4),)),
+    (23, ((10, 4, 4), (10, 7, 7))),
     (26, ((0, 9, 13), (3, 11, 14))),
     (27, ((1, 8, 14),)),
     (30, ((4, 8, 11),)),
@@ -90,7 +90,7 @@ def build(counts, cores, topo):
     first, second = {}, {}
     expect = {c: {"staged": 0, "arrived": 0, "sent": 0} for c in range(32)}
     for c in range(32):
-        first[c] = pack(seg_w[c], c, topo) + pack(own_w[c], c, topo)
+        first[c] = pack(seg_w[c] + own_w[c], c, topo)
         second[c] = pack(out_w[c], c, topo)
         for call in first[c] + second[c]:
             for w, mask in call:

from concourse.bass import DstId, RemoteDMATransfer

SCRATCH = {
    "xs": ("sbuf", [128, 116], "float32"),
    "stage": ("sbuf", [128, 88], "float32"),
    "land": ("sbuf", [128, 480], "float32"),
}
SEMAPHORES = ["loaded", "staged", "arrived", "stored", "sent"]

RELAYS = (
    (2, ((8, 3, 5), (9, 5, 7))),
    (3, ((8, 0, 2), (8, 7, 7))),
    (6, ((12, 1, 5), (13, 5, 6))),
    (7, ((12, 7, 7), (14, 7, 7), (13, 0, 2), (15, 0, 1))),
    (24, ((10, 5, 5), (11, 5, 7))),
    (25, ((10, 1, 3), (11, 3, 4))),
    (28, ((14, 0, 5), (15, 5, 7))),
    (29, ((15, 2, 3),)),
    (19, ((9, 1, 4),)),
    (23, ((10, 4, 4), (10, 7, 7))),
    (26, ((0, 9, 13), (3, 11, 14))),
    (27, ((1, 8, 14),)),
    (30, ((4, 8, 11),)),
    (31, ((4, 12, 15), (5, 8, 8))),
    (0, ((2, 9, 13),)),
    (1, ((3, 8, 10),)),
    (4, ((6, 8, 11), (7, 11, 12))),
    (5, ((6, 12, 15),)),
    (10, ((5, 9, 12),)),
    (15, ((5, 13, 15),)),
)

CACHE = {}


def pack(writes, src, topo):
    groups = []
    for w in writes:
        key = (topo.chip(w[0]) != topo.chip(src), w[5])
        for grp in groups:
            if grp[0] == key:
                grp[1].append(w)
                break
        else:
            groups.append((key, [w]))
    calls = []
    for (off, _), ws in groups:
        cap = 8 if off else 16
        while ws:
            k = 1
            while k * 2 <= min(len(ws), 8):
                k *= 2
            e = cap // k
            calls.append([(w, ((1 << e) - 1) << (i * e)) for i, w in enumerate(ws[:k])])
            ws = ws[k:]
    return calls


def build(counts, cores, topo):
    n = len(cores)
    xoff = [[sum(counts[s][:d]) for d in range(n)] for s in range(n)]
    yoff = [[sum(counts[q][d] for q in range(s)) for s in range(n)] for d in range(n)]
    seg_w = {c: [] for c in range(32)}
    own_w = {c: [] for c in range(32)}
    out_w = {c: [] for c in range(32)}
    todo = set((s, d) for s in range(n) for d in range(n)
               if counts[s][d] and topo.chip(cores[s]) != topo.chip(cores[d]))
    for s in range(n):
        for d in range(n):
            if counts[s][d] and s != d and (s, d) not in todo:
                own_w[cores[s]].append([cores[d], "land", yoff[d][s], "xs", xoff[s][d], counts[s][d], "arrived"])
    for relay, segs in RELAYS:
        col = 0
        for s, a, b in segs:
            width = sum(counts[s][a:b + 1])
            seg_w[cores[s]].append([relay, "stage", col, "xs", xoff[s][a], width, "staged"])
            for d in range(a, b + 1):
                c = counts[s][d]
                if c == 0:
                    continue
                todo.remove((s, d))
                last = out_w[relay][-1] if out_w[relay] else None
                if last and last[0] == cores[d] and last[2] + last[5] == yoff[d][s] and last[4] + last[5] == col:
                    last[5] += c
                else:
                    out_w[relay].append([cores[d], "land", yoff[d][s], "stage", col, c, "arrived"])
                col += c
    if todo:
        raise ValueError("RELAYS leaves pieces out: %s" % sorted(todo))
    first, second = {}, {}
    expect = {c: {"staged": 0, "arrived": 0, "sent": 0} for c in range(32)}
    for c in range(32):
        first[c] = pack(seg_w[c] + own_w[c], c, topo)
        second[c] = pack(out_w[c], c, topo)
        for call in first[c] + second[c]:
            for w, mask in call:
                e = bin(mask).count("1")
                expect[w[0]][w[6]] += e
                expect[c]["sent"] += e
    return first, second, expect, xoff, yoff


def rank_program(g, core, T, topo):
    counts = T.tables["COUNTS"]
    cores = list(T.cores)
    n = len(cores)
    if "plan" not in CACHE:
        CACHE["plan"] = build(counts, cores, topo)
    first, second, expect, xoff, yoff = CACHE["plan"]
    rank = T.rank_of(core)
    arrived = expect[core]["arrived"]

    def issue(calls):
        for call in calls:
            if len(call) == 1:
                (dst, ob, oc, ib, ic, width, sem), mask = call[0]
                rid, pid, _ = topo.addr(dst)
                g.remote_dma(T[ob][:, oc:oc + width], T[ib][:, ic:ic + width], T.sem[sem], T.sem.sent, pid, rid, mask)
                continue
            transfers = []
            for (dst, ob, oc, ib, ic, width, sem), mask in call:
                rid, pid, _ = topo.addr(dst)
                transfers.append(RemoteDMATransfer(dst_ids=[DstId(rid=rid, pnc=pid)], dma_engine_mask=mask,
                                                   remote_sem=T.sem[sem], src=T[ib][:, ic:ic + width],
                                                   dst=T[ob][:, oc:oc + width]))
            g.remote_dma_fused(transfers, local_sem=T.sem.sent)

    if rank is not None:
        used = sum(counts[rank])
        g.sync.dma_start(T.xs[:, 0:used], T.x[:, 0:used]).then_inc(T.sem.loaded, 16)
        c = counts[rank][rank]
        if c:
            g.scalar.dma_start(T.land[:, yoff[rank][rank]:yoff[rank][rank] + c],
                               T.x[:, xoff[rank][rank]:xoff[rank][rank] + c]).then_inc(T.sem.arrived, 16)
            arrived += 16
        g.wait_ge(T.sem.loaded, 16)
        issue(first[core])

    if second[core]:
        g.wait_ge(T.sem.staged, expect[core]["staged"])
        issue(second[core])

    if rank is not None:
        owed = sum(counts[s][rank] for s in range(n))
        g.wait_ge(T.sem.arrived, arrived)
        g.dma_start(T.y[:, 0:owed], T.land[:, 0:owed]).then_inc(T.sem.stored, 16)
        g.wait_ge(T.sem.stored, 16)

    if expect[core]["sent"]:
        g.wait_ge(T.sem.sent, expect[core]["sent"])
